import numpy as np
import ml_dtypes


def mxq(x, axis, fmt="e4m3"):
    dtype, down = {"e4m3": (ml_dtypes.float8_e4m3fn, 7), "e5m2": (ml_dtypes.float8_e5m2, 14)}[fmt]
    v = np.moveaxis(np.asarray(x, np.float32).astype(ml_dtypes.bfloat16).astype(np.float64), axis, -1)
    blocks = v.reshape(v.shape[:-1] + (-1, 32))
    amax = np.abs(blocks).max(-1, keepdims=True)
    byte = np.maximum(np.where(amax > 0, np.frexp(amax)[1] - 1 + 127, 0) - down, 1)
    scale = np.exp2(byte - 127.0)
    codes = (blocks / scale).astype(np.float32).astype(dtype).astype(np.float64)
    return np.moveaxis((codes * scale).reshape(v.shape), -1, axis)


WIDE = False


def mx_kscale(k):
    if not WIDE:
        return np.ones(k)
    levels = np.array([10, -10, 5, -5, 0])
    if k % 512:
        return np.exp2(np.random.permutation(np.resize(levels, k // 32))).repeat(32)
    a = np.empty((k // 512, 16))
    for p in range(k // 512):
        a[p, :8] = np.random.permutation(np.resize(levels, 8))
        for g in range(8):
            far = levels[np.abs(levels - a[p, g]) >= 10]
            a[p, g + 8] = far[np.random.randint(len(far))]
    return np.exp2(a.ravel()).repeat(32)


BF16 = ml_dtypes.bfloat16


def bf(x):
    return np.asarray(x, np.float32).astype(BF16)


def f64(x):
    return np.asarray(x).astype(np.float64)


M, K, F, N = 2048, 1024, 1024, 1024


def draw0():
    s = mx_kscale(K)
    u = mx_kscale(M)
    x = np.random.standard_normal((M, K)) * s
    c = np.random.standard_normal((K, F)) / np.sqrt(K) / s[:, None]
    offset = 0.4 * np.random.standard_normal(F)
    gain = -(1.0 + 0.3 * np.random.standard_normal(M)) * u
    bmat = np.random.standard_normal((N, M)) / np.sqrt(M) / u
    return {"x": bf(x),
            "c": bf(c),
            "offset": bf(offset),
            "gain": bf(gain),
            "bmat": bf(bmat)}


def core(x, c, offset, gain, bmat):
    sigma = mxq(f64(x), 1, "e4m3") @ mxq(f64(c), 0, "e4m3")
    ctrl = f64(gain)[:, None] * np.tanh(sigma + f64(offset))
    v = mxq(f64(bmat), 1, "e4m3") @ mxq(ctrl, 0, "e4m3")
    return v


def e4m3fn_bytes(y):
    return np.clip(np.asarray(y, np.float64), -448.0, 448.0).astype(np.float32).astype(ml_dtypes.float8_e4m3fn).view(np.uint8)


def e4m3fn_values(b):
    return np.asarray(b, np.uint8).view(ml_dtypes.float8_e4m3fn).astype(np.float64)


def setup_inputs():
    d = draw0()
    x0 = np.asarray(d['x']).astype(np.float64)
    s = (np.max(np.abs(x0), axis=(0,), keepdims=True) / 448.0).astype(np.float32)
    out = {}
    for k, v in d.items():
        if k == 'x':
            out['x_bytes'] = e4m3fn_bytes(x0 / s.astype(np.float64))
            out['x_scale'] = s
        else:
            out[k] = v
    return out


def reference(x_bytes, x_scale, c, offset, gain, bmat):
    return core(e4m3fn_values(x_bytes) * x_scale.astype(np.float64), c, offset, gain, bmat)

from contextlib import ExitStack

import concourse.mybir as mybir
from concourse.masks import make_identity

M, K, F, N = 2048, 1024, 1024, 1024
FLOPS = 2 * M * K * F + 2 * N * M * F

F32 = mybir.dt.float32
BF16 = mybir.dt.bfloat16
U32 = mybir.dt.uint32
U8 = mybir.dt.uint8
FP8 = mybir.dt.float8_e4m3fn
FP8X4 = mybir.dt.float8_e4m3fn_x4
ACT = mybir.ActivationFunctionType
MULT = mybir.AluOpType.mult

P = 128
G = M // 512
Q = K // 512
FT = F // P
NT = N // P
CH = 4
FC = F // CH
FPC = FC // P


def tile_networked_sliding_control_s7_kernel(tc, x_bytes, x_scale, c, offset, gain, bmat, out):
    nc = tc.nc
    with ExitStack() as ctx:
        const = ctx.enter_context(tc.tile_pool(name="const", bufs=1))
        pool = ctx.enter_context(tc.tile_pool(name="work", bufs=2))
        psum = ctx.enter_context(tc.psum_pool(name="psum", bufs=4))

        x_view = x_bytes.rearrange("(g p t) k -> g p t k", p=P, t=4)
        c_view = c.rearrange("(q p j) (h f) -> q h p j f", p=P, j=4, h=2)
        b_view = bmat.rearrange("(n p) m -> n p m", p=P)
        x_raw, c_raw, b_raw = {}, {}, {}

        def load_x(g, parts=1):
            xbytes = pool.tile([P, 4, K], U8, bufs=3, name="xbytes")
            step = 4 // parts
            x_raw[g] = xbytes
            return [lambda i=i: nc.sync.dma_start(out=xbytes[:, i * step : (i + 1) * step, :], in_=x_view[g][:, i * step : (i + 1) * step, :]) for i in range(parts)]

        def load_c(q, h):
            raw = pool.tile([P, 4, 512], BF16, bufs=7, name="raw")
            nc.sync.dma_start(out=raw[:], in_=c_view[q, h])
            c_raw[q, h] = raw

        def load_b(n):
            raw = pool.tile([P, 4, 512], BF16, bufs=7, name="raw")
            nc.sync.dma_start(out=raw[:].rearrange("p a b -> p (a b)"), in_=b_view[n])
            b_raw[n] = raw

        c_int, c_codes, x_codes, b_codes, k_codes = {}, {}, {}, {}, {}
        x_wide, x_tp, x_int, b_tp, b_int = {}, {}, {}, {}, {}

        def c_inter(q, h, eng):
            cint = pool.tile([P, 512, 4], BF16, bufs=2, name="cint", align_bytes=64)
            dst = cint[:].rearrange("p (c i) t -> p c t i", i=4)
            src = c_raw[q, h][:].rearrange("p t (c i) -> p c t i", i=4)
            if eng == "v":
                nc.vector.tensor_copy(out=dst, in_=src)
            else:
                nc.scalar.copy(out=dst, in_=src)
            c_int[q, h] = cint

        def c_quant(q, h):
            codes = const.tile([P, 512], U32, name=f"cc{q}{h}", align_bytes=64)
            scales = const.tile([P, 512], U8, name=f"cs{q}{h}", align_bytes=64)
            nc.vector.quantize_mx(out=codes[:].bitcast(FP8X4), scales=scales[:], in_=c_int[q, h][:].rearrange("p f t -> p (f t)"))
            c_codes[q, h] = (codes, scales)

        def widen(g, t):
            xw = pool.tile([P, K], BF16, bufs=3, name="xw")
            nc.vector.tensor_tensor(out=xw[:], in0=x_raw[g][:, t, :].bitcast(FP8), in1=scale_b[:], op=MULT)
            x_wide[g, t] = xw

        def x_turn(g, t):
            words = x_wide[g, t][:].bitcast(F32)
            tp = psum.tile([P, 4, P], F32, name="tp")
            for q in range(Q):
                for u in range(2):
                    nc.tensor.transpose(tp[:, 2 * q + u, :], words[:, 256 * q + u : 256 * (q + 1) : 2], ident[:])
            x_tp[g, t] = tp

        def x_copy(g, t):
            if t == 0:
                xint = pool.tile([P, Q, 512, 4], BF16, bufs=2, name="xint", align_bytes=64)
                x_int[g] = xint
            view = x_int[g][:].rearrange("p q r j -> p (q r j)").bitcast(F32).rearrange("p (q r u) -> p q r u", q=Q, u=2)
            nc.scalar.copy(out=view[:, :, t * P : (t + 1) * P, :], in_=x_tp[g, t][:].rearrange("p (q u) r -> p q r u", u=2))

        def x_quant(g):
            codes = const.tile([P, Q, 512], U32, name=f"xc{g}", align_bytes=64)
            scales = const.tile([P, Q, 512], U8, name=f"xs{g}", align_bytes=64)
            nc.vector.quantize_mx(
                out=codes[:].rearrange("p q r -> p (q r)").bitcast(FP8X4),
                scales=scales[:].rearrange("p q r -> p (q r)"),
                in_=x_int[g][:].rearrange("p q r j -> p (q r j)"),
            )
            x_codes[g] = (codes, scales)

        def b_turn(n, half):
            words = b_raw[n][:].rearrange("p a b -> p (a b)").bitcast(F32)
            tp = psum.tile([P, 4, P], F32, name="tp")
            for gl in range(2):
                g = 2 * half + gl
                for u in range(2):
                    nc.tensor.transpose(tp[:, 2 * gl + u, :], words[:, 256 * g + u : 256 * (g + 1) : 2], ident[:])
            b_tp[n, half] = tp

        def b_copy(n, half, eng):
            if half == 0:
                bint = pool.tile([P, G, P, 4], BF16, bufs=2, name="bint", align_bytes=64)
                b_int[n] = bint
            view = b_int[n][:].rearrange("p g r j -> p (g r j)").bitcast(F32).rearrange("p (g r u) -> p g r u", g=G, u=2)
            dst = view[:, 2 * half : 2 * half + 2, :, :]
            src = b_tp[n, half][:].rearrange("p (g u) r -> p g r u", u=2)
            if eng == "v":
                nc.vector.tensor_copy(out=dst, in_=src)
            else:
                nc.scalar.copy(out=dst, in_=src)

        def b_quant(n):
            codes = const.tile([P, G, P], U32, name=f"bc{n}", align_bytes=64)
            scales = const.tile([P, G, P], U8, name=f"bs{n}", align_bytes=64)
            nc.vector.quantize_mx(
                out=codes[:].rearrange("p g r -> p (g r)").bitcast(FP8X4),
                scales=scales[:].rearrange("p g r -> p (g r)"),
                in_=b_int[n][:].rearrange("p g r j -> p (g r j)"),
            )
            b_codes[n] = (codes, scales)

        s_ps, tanh_t, k_wide, k_tp, k_int = {}, {}, {}, {}, {}

        def sigma(g, ft):
            ps = psum.tile([P, 512], F32, name="mm")
            h, col = ft // 4, slice((ft % 4) * P, (ft % 4 + 1) * P)
            xc, xs = x_codes[g]
            for q in range(Q):
                cc, cs = c_codes[q, h]
                nc.tensor.matmul_mx(
                    out=ps[:],
                    lhsT=cc[:, col].bitcast(FP8X4),
                    lhsT_scale=cs[:, col],
                    rhs=xc[:, q, :].bitcast(FP8X4),
                    rhs_scale=xs[:, q, :],
                    start=(q == 0),
                    stop=(q == Q - 1),
                )
            s_ps[g, ft] = ps

        def tanh(g, ft):
            th = pool.tile([P, 512], F32, bufs=28, name="th")
            nc.scalar.activation(out=th[:], in_=s_ps[g, ft][:], func=ACT.Tanh, bias=off_cols[:, ft : ft + 1])
            tanh_t[g, ft] = th

        def k_gain(g, ft):
            kw = pool.tile([P, 512], BF16, bufs=6, name="kw")
            nc.vector.tensor_tensor(
                out=kw[:].rearrange("f (u p e) -> f u p e", u=2, e=2),
                in0=tanh_t[g, ft][:].rearrange("f (u e p) -> f u p e", u=2, e=2),
                in1=gain_b[:, 512 * g : 512 * (g + 1)].rearrange("f (p u e) -> f u p e", u=2, e=2),
                op=MULT,
            )
            k_wide[g, ft] = kw

        def k_turn(g, ch):
            tp = psum.tile([P, 4, P], F32, name="tp")
            for i in range(FPC):
                words = k_wide[g, ch * FPC + i][:].bitcast(F32)
                for u in range(2):
                    nc.tensor.transpose(tp[:, 2 * i + u, :], words[:, P * u : P * (u + 1)], ident[:])
            k_tp[g, ch] = tp

        def k_copy(g, ch):
            kint = pool.tile([P, FPC, P, 4], BF16, bufs=3, name="kint", align_bytes=64)
            view = kint[:].rearrange("p i f j -> p (i f j)").bitcast(F32).rearrange("p (i f u) -> p i f u", i=FPC, u=2)
            nc.scalar.copy(out=view, in_=k_tp[g, ch][:].rearrange("p (i u) f -> p i f u", u=2))
            k_int[g, ch] = kint

        def k_quant(g, ch):
            codes = const.tile([P, FC], U32, name=f"kc{g}_{ch}", align_bytes=64)
            scales = const.tile([P, FC], U8, name=f"ks{g}_{ch}", align_bytes=64)
            nc.vector.quantize_mx(out=codes[:].bitcast(FP8X4), scales=scales[:], in_=k_int[g, ch][:].rearrange("p i f j -> p (i f j)"))
            k_codes[g, ch] = (codes, scales)

        def second(ch, pair, eng):
            ps = psum.tile([P, 2, FC], F32, name="mm")
            for i in range(2):
                bc, bs = b_codes[2 * pair + i]
                for g in range(G):
                    kc, ks = k_codes[g, ch]
                    nc.tensor.matmul_mx(
                        out=ps[:, i, :],
                        lhsT=bc[:, g, :].bitcast(FP8X4),
                        lhsT_scale=bs[:, g, :],
                        rhs=kc[:].bitcast(FP8X4),
                        rhs_scale=ks[:],
                        start=(g == 0),
                        stop=(g == G - 1),
                    )
            vo = pool.tile([P, 2, FC], F32, bufs=3, name="vo")
            if eng == "s":
                nc.scalar.copy(out=vo[:], in_=ps[:])
            else:
                nc.vector.tensor_copy(out=vo[:], in_=ps[:])
            nc.sync.dma_start(
                out=out[2 * pair * P : 2 * (pair + 1) * P, ch * FC : (ch + 1) * FC].rearrange("(i p) f -> p i f", i=2),
                in_=vo[:],
            )

        ident = const.tile([P, P], F32)
        make_identity(nc, ident[:])
        off_rows = const.tile([P, P], BF16)
        nc.gpsimd.memset(off_rows[:], 0.0)
        warm = const.tile([P, 1], F32)
        nc.gpsimd.memset(warm[:], 0.0)
        warm_out = const.tile([P, 1], F32)
        scale_b = const.tile([P, K], F32)
        gain_b = const.tile([P, M], BF16)
        scale_v = const.tile([P, 8], F32)
        off_f = const.tile([P, P], F32)
        off_cols = const.tile([P, FT], F32)

        nc.scalar.dma_start(out=scale_v[:], in_=x_scale.rearrange("o (p m) -> (o p) m", m=8))
        nc.scalar.activation(out=warm_out[:], in_=warm[:], func=ACT.Tanh)
        x0 = load_x(0, 2)
        x0[0]()
        x0[1]()
        load_c(0, 0)
        load_c(1, 0)
        load_b(0)
        nc.scalar.dma_start(out=off_rows[0:FT, :], in_=offset.rearrange("(c p) -> c p", p=P))
        load_b(1)
        load_b(2)
        load_b(3)
        load_b(4)
        load_x(1)[0]()
        load_c(0, 1)
        load_c(1, 1)
        load_x(2)[0]()
        load_b(5)
        load_b(6)
        load_b(7)
        nc.scalar.dma_start(out=gain_b[:], in_=gain.partition_broadcast(P))
        for half in range(2):
            sp = psum.tile([P, 4, P], F32, name="tp")
            for i in range(4):
                nc.tensor.transpose(sp[:, i, :], scale_v[:, 4 * half + i : 4 * half + i + 1].to_broadcast([P, P]), ident[:])
            dst = scale_b[:].rearrange("p (n m) -> p n m", m=8)[:, :, 4 * half : 4 * half + 4]
            if half:
                nc.vector.tensor_copy(out=dst, in_=sp[:].rearrange("p m n -> p n m"))
            else:
                nc.scalar.copy(out=dst, in_=sp[:].rearrange("p m n -> p n m"))

        def prep_x(g):
            for t in range(4):
                widen(g, t)
                x_turn(g, t)
                x_copy(g, t)
            x_quant(g)

        def prep_b(n, e0="s", e1="s"):
            for half in range(2):
                b_turn(n, half)
                b_copy(n, half, e1 if half else e0)
            b_quant(n)

        def ctrl(g, ch):
            for i in range(FPC):
                k_gain(g, ch * FPC + i)
            k_turn(g, ch)
            k_copy(g, ch)
            k_quant(g, ch)

        def off_prep():
            nc.scalar.copy(out=off_f[:], in_=off_rows[:])
            off_ps = psum.tile([P, 4, P], F32, name="tp")
            nc.tensor.transpose(off_ps[:, 0, :], off_f[:], ident[:])
            nc.scalar.copy(out=off_cols[:], in_=off_ps[:, 0, 0:FT])

        prep_b(0, "s", "v")
        c_inter(0, 0, "v")
        for t in range(4):
            widen(0, t); x_turn(0, t); x_copy(0, t)
        c_inter(1, 0, "s")
        c_quant(0, 0)
        x_quant(0)
        c_quant(1, 0)
        off_prep()
        prep_b(1, "s", "s")
        prep_b(2, "s", "s")
        c_inter(0, 1, "v")
        c_inter(1, 1, "s")
        c_quant(0, 1)
        c_quant(1, 1)
        for g in range(G):
            for ft in range(FT):
                sigma(g, ft)
                tanh(g, ft)
            if g + 1 < G:
                prep_x(g + 1)
            ctrl(g, 0)
            if g == 0:
                load_x(3)[0]()
            for n in {0: (3, 4), 1: (5, 6), 2: (7,), 3: ()}[g]:
                prep_b(n, "s", "s")
        for ch in range(1, CH):
            for g in range(G):
                ctrl(g, ch)
            for pair in range(NT // 2):
                second(ch - 1, pair, "s")
        for pair in range(NT // 2):
            second(CH - 1, pair, "s" if pair % 2 else "v")
